import numpy as np
import ml_dtypes


def mxq(x, axis, fmt="e4m3"):
    dtype, down = {"e4m3": (ml_dtypes.float8_e4m3fn, 7), "e5m2": (ml_dtypes.float8_e5m2, 14)}[fmt]
    v = np.moveaxis(np.asarray(x, np.float32).astype(ml_dtypes.bfloat16).astype(np.float64), axis, -1)
    blocks = v.reshape(v.shape[:-1] + (-1, 32))
    amax = np.abs(blocks).max(-1, keepdims=True)
    byte = np.maximum(np.where(amax > 0, np.frexp(amax)[1] - 1 + 127, 0) - down, 1)
    scale = np.exp2(byte - 127.0)
    codes = (blocks / scale).astype(np.float32).astype(dtype).astype(np.float64)
    return np.moveaxis((codes * scale).reshape(v.shape), -1, axis)


WIDE = False


def mx_kscale(k):
    if not WIDE:
        return np.ones(k)
    levels = np.array([10, -10, 5, -5, 0])
    if k % 512:
        return np.exp2(np.random.permutation(np.resize(levels, k // 32))).repeat(32)
    a = np.empty((k // 512, 16))
    for p in range(k // 512):
        a[p, :8] = np.random.permutation(np.resize(levels, 8))
        for g in range(8):
            far = levels[np.abs(levels - a[p, g]) >= 10]
            a[p, g + 8] = far[np.random.randint(len(far))]
    return np.exp2(a.ravel()).repeat(32)


def f64(x):
    return np.asarray(x).astype(np.float64)


def striped(idx):
    return np.tile(idx.reshape(-1, 16).T, (8, 1)).astype(np.uint16)


def unstriped(offs):
    return offs[:16].T.reshape(-1).astype(np.int64)


E2M1 = np.array([0.0, 0.5, 1.0, 1.5, 2.0, 3.0, 4.0, 6.0, -0.0, -0.5, -1.0, -1.5, -2.0, -3.0, -4.0, -6.0])


def pack_weight(w, fmt):
    k, n = w.shape
    w = f64(np.asarray(w, np.float32).astype(ml_dtypes.bfloat16)).reshape(k // 32, 32, n)
    amax = np.abs(w).max(1)
    if fmt == "e4m3":
        byte = np.frexp(amax)[1] - 1 + 127 - 7
    else:
        mant, ex = np.frexp(amax / 6.0)
        byte = np.where(mant > 0.5, ex, ex - 1) + 127
    byte = np.clip(np.where(amax > 0, byte, 1), 1, 254)
    scaled = (w * np.exp2(127.0 - byte)[:, None, :]).reshape(k, n).astype(np.float32)
    by_word = np.ascontiguousarray(scaled.reshape(k // 512, 128, 4, n).transpose(0, 1, 3, 2))
    if fmt == "e4m3":
        words = by_word.astype(ml_dtypes.float8_e4m3fn).view(np.uint8)
    else:
        c = by_word.astype(ml_dtypes.float4_e2m1fn).view(np.uint8) & 0xF
        words = (c[..., 0::2] | (c[..., 1::2] << 4)).reshape(k // 512, 128, 2 * n)
    return np.ascontiguousarray(words), np.ascontiguousarray(byte.astype(np.uint8).reshape(k // 512, 16, n))


def unpack_weight(words, scales, fmt):
    g, _, n = scales.shape
    words = np.ascontiguousarray(words).reshape(g, 128, n, -1)
    if fmt == "e4m3":
        vals = words.view(ml_dtypes.float8_e4m3fn).astype(np.float64)
    else:
        nib = np.empty((g, 128, n, 4), np.uint8)
        nib[..., 0::2] = words & 0xF
        nib[..., 1::2] = words >> 4
        vals = E2M1[nib]
    vals = vals * np.repeat(np.exp2(scales.astype(np.float64) - 127.0), 8, axis=1)[..., None]
    return vals.transpose(0, 1, 3, 2).reshape(g * 512, n)


def gelu(v):
    return 0.5 * v * (1.0 + np.tanh(np.sqrt(2.0 / np.pi) * (v + 0.044715 * v**3)))


def striped8(idx):
    return np.concatenate([v.reshape(-1, 16).T for v in idx]).astype(np.uint16)


def unstriped8(offs):
    return np.stack([offs[16 * g:16 * g + 16].T.reshape(-1) for g in range(8)]).astype(np.int64)


def runs(v, idx8):
    k = np.arange(v.shape[0])
    return v[k[:, None], idx8[k % 512 // 64]]


def often(T, S):
    return np.random.permutation(T)[(T * np.random.uniform(0, 1, S) ** 4).astype(np.int64)]


K, T, S, H, P, N = 1536, 2048, 1024, 1024, 512, 384

def setup_inputs():
    n = np.random.standard_normal
    s = mx_kscale(K)[:, None]
    u = mx_kscale(H)[:, None]
    d = {}
    d["tab_words"], d["tab_scales"] = pack_weight(n((K, T)) * s, "e4m3")
    d["offs"] = striped8(np.stack([often(T, S) for _ in range(8)]))
    d["pos1"] = striped(np.random.permutation(S)[:P])
    d["pos2"] = striped(np.random.permutation(S)[:P])
    d["w1"] = (1.5 * n((K, H)) / K**0.5 / s).astype(np.float32)
    d["b1"] = (0.6 * n(H)).astype(np.float32)
    d["gain"] = (np.exp(0.3 * n(H)) * u[:, 0]).astype(np.float32)
    d["wd_words"], d["wd_scales"] = pack_weight(1.8 * n((H, N)) / H**0.5 / u, "e2m1")
    d["wm"] = (1.1 * n((H, N)) / H**0.5 / u).astype(np.float32)
    return d

def reference(tab_words, tab_scales, offs, pos1, pos2, w1, b1, gain, wd_words, wd_scales, wm):
    v = runs(unpack_weight(tab_words, tab_scales, "e4m3"), unstriped8(offs))
    lin = mxq(f64(w1), 0, "e4m3").T @ v
    h = f64(gain)[:, None] * np.tanh(lin + f64(b1)[:, None])
    h1 = h[:, unstriped(pos1)]
    h2 = h[:, unstriped(pos2)]
    diff = mxq(h1 - h2, 0, "e4m3")
    low = mxq(np.minimum(h1, h2), 0, "e4m3")
    y1 = unpack_weight(wd_words, wd_scales, "e2m1").T @ diff
    y2 = mxq(f64(wm), 0, "e4m3").T @ low
    return np.log(1.0 + np.abs(y1)) + y2

@@ -1,0 +1,271 @@
+from contextlib import ExitStack
+
+import concourse.mybir as mybir
+
+K, T, S, H, PAIRS, N = 1536, 2048, 1024, 1024, 512, 384
+FLOPS = 2 * K * H * S + 2 * 2 * H * N * PAIRS
+
+F32 = mybir.dt.float32
+BF16 = mybir.dt.bfloat16
+I32 = mybir.dt.int32
+U32 = mybir.dt.uint32
+U16 = mybir.dt.uint16
+U8 = mybir.dt.uint8
+FP8X4 = mybir.dt.float8_e4m3fn_x4
+FP4X4 = mybir.dt.float4_e2m1fn_x4
+ALU = mybir.AluOpType
+ACT = mybir.ActivationFunctionType
+
+P = 128
+PACK = 4
+K_PASS = P * PACK
+K_PASSES = K // K_PASS
+H_PASSES = H // K_PASS
+BANK = 512
+N_SLICES = N // P
+CHUNK = 128
+VECTOR_GAIN_SLICES = 2
+
+
+def tile_list_deed_defect_scores_kernel(
+    tc, tab_words, tab_scales, offs, pos1, pos2, w1, b1, gain, wd_words, wd_scales, wm, out
+):
+    nc = tc.nc
+    with ExitStack() as ctx:
+        keep = ctx.enter_context(tc.tile_pool(name="keep", bufs=1))
+        stage = ctx.enter_context(tc.tile_pool(name="stage", bufs=5))
+        work = ctx.enter_context(tc.tile_pool(name="work", bufs=2))
+        psum = ctx.enter_context(tc.psum_pool(name="psum", bufs=1))
+
+        offs_sb = keep.tile([P, S // 16], U16, name="offs_sb")
+        pos1_sb = keep.tile([P, PAIRS // 16], U16, name="pos1_sb")
+        pos2_sb = keep.tile([P, PAIRS // 16], U16, name="pos2_sb")
+
+        nc.sync.dma_start(offs_sb[:], offs)
+        nc.sync.dma_start(pos1_sb[:], pos1)
+        nc.sync.dma_start(pos2_sb[:], pos2)
+        scale_window = stage.tile([P, T], U8, name="scale_window", tag="raw", align_bytes=64)
+        nc.vector.memset(scale_window[:].bitcast(I32), 0)
+        for a in range(K_PASSES):
+            rows = tab_scales[a].bitcast(I32).rearrange("(g e) c -> e g c", e=2)
+            for e in range(2):
+                nc.scalar.dma_start(out=scale_window[4 * a + e : P : 16, :].bitcast(I32), in_=rows[e])
+        warm_in = stage.tile([P, 1], F32, name="warm_in", tag="raw", align_bytes=64)
+        warm_out = stage.tile([P, 1], F32, name="warm_out", tag="raw", align_bytes=64)
+        nc.vector.memset(warm_in[:], 0.0)
+        nc.scalar.activation(warm_out[:], warm_in[:], ACT.Tanh)
+
+        def load_table(a):
+            words = stage.tile([P, T], U32, name="words", tag="raw", align_bytes=64)
+            nc.sync.dma_start(
+                out=words[:].bitcast(I32), in_=tab_words[a].rearrange("p t i -> p (t i)").bitcast(I32)
+            )
+            return words
+
+        def load_rows(src):
+            raw = stage.tile([P, PACK, src.shape[1]], F32, name="raw", tag="raw", align_bytes=64)
+            nc.sync.dma_start(out=raw[:], in_=src.rearrange("(p j) c -> p j c", j=PACK))
+            return raw
+
+        def load_w1(a, b):
+            return load_rows(w1[K_PASS * a : K_PASS * (a + 1), K_PASS * b : K_PASS * (b + 1)])
+
+        tables = [load_table(0), load_table(1)]
+
+        bias_sb = keep.tile([P, H_PASSES, PACK], F32, name="bias_sb")
+        gain_sb = keep.tile([P, H_PASSES, PACK], F32, name="gain_sb")
+        nc.gpsimd.dma_start(out=bias_sb[:], in_=b1.rearrange("(b p t) -> p b t", p=P, t=PACK))
+        nc.gpsimd.dma_start(out=gain_sb[:], in_=gain.rearrange("(b p t) -> p b t", p=P, t=PACK))
+        wd_planes = keep.tile([P, H_PASSES, N], U8, name="wd_planes", align_bytes=64)
+        nc.gpsimd.memset(wd_planes[:].bitcast(I32), 0)
+        for d in range(4):
+            nc.gpsimd.dma_start(
+                out=wd_planes[32 * d : 32 * d + 4].bitcast(I32),
+                in_=wd_scales[:, 4 * d : 4 * d + 4, :].rearrange("b r c -> r b c").bitcast(I32),
+            )
+
+        picked_scales = keep.tile([P, S], U8, name="picked_scales", align_bytes=64)
+        nc.vector.tensor_copy(picked_scales[:], scale_window[:].indirect(offs_sb[:]))
+        table_planes = keep.tile([P, S], U8, name="table_planes", align_bytes=64)
+        nc.vector.tensor_copy(table_planes[:].bitcast(I32), picked_scales[:].bitcast(I32))
+        for e in range(2):
+            nc.scalar.dma_start(
+                out=table_planes[2 + e : P - 16 : 4, :].bitcast(I32),
+                in_=picked_scales[16 + e : P : 4, :].bitcast(I32),
+            )
+
+        def gather_table(a):
+            picked = keep.tile([P, S], U32, name=f"picked{a}", align_bytes=64)
+            nc.vector.tensor_copy(picked[:], tables[a][:].indirect(offs_sb[:]))
+            return picked
+
+        def round_w1(raw, t0, t1, copy, name):
+            grouped = work.tile([P, (t1 - t0) * K_PASS], BF16, name=name, tag=name, align_bytes=64)
+            copy(
+                grouped[:].rearrange("p (t m j) -> p m j t", m=P, j=PACK),
+                raw[:].rearrange("p j (m t) -> p m j t", t=PACK)[:, :, :, t0:t1],
+            )
+            return grouped
+
+        def quantize(grouped, name):
+            width = grouped.shape[1] // PACK
+            codes = keep.tile([P, width], U32, name=name + "_codes", align_bytes=64)
+            scales = keep.tile([P, width], U8, name=name + "_scales", align_bytes=64)
+            nc.vector.quantize_mx(out=codes[:].bitcast(FP8X4), scales=scales[:], in_=grouped[:])
+            return codes, scales
+
+        def columns(operand, c0, c1):
+            return operand[0][:, c0:c1], operand[1][:, c0:c1]
+
+        w1q = {}
+
+        def split_w1(a, raw):
+            low_half = round_w1(raw, 0, 2, nc.vector.tensor_copy, "w1_v")
+            high_half = round_w1(raw, 2, 4, nc.scalar.copy, "w1_s")
+            for t0, half in ((0, low_half), (2, high_half)):
+                operand = quantize(half, f"w1_{a}_0_{t0}")
+                for t in range(2):
+                    w1q[a, 0, t0 + t] = columns(operand, P * t, P * (t + 1))
+
+        picked = [gather_table(0), gather_table(1)]
+        split_w1(0, load_w1(0, 0))
+        tables.append(load_table(2))
+        picked.append(gather_table(2))
+        split_w1(1, load_w1(1, 0))
+        split_w1(2, load_w1(2, 0))
+
+        def bank(i):
+            return psum.tile([P, BANK], F32, name=f"bank{i}", tag=f"bank{i}")
+
+        def first_pass(acc, a, b, t, half):
+            cols = slice(BANK * half, BANK * (half + 1))
+            nc.tensor.matmul_mx(
+                out=acc[:],
+                lhsT=w1q[a, b, t][0].bitcast(FP8X4),
+                lhsT_scale=w1q[a, b, t][1],
+                rhs=picked[a][:, cols].bitcast(FP8X4),
+                rhs_scale=table_planes[4 * a : P, cols],
+                start=(a == 0),
+                stop=(a == K_PASSES - 1),
+            )
+
+        def features(accs, b, t, on_vector):
+            bounded = work.tile([P, S], F32, name="bounded", tag="bounded")
+            h = keep.tile([P, S], F32, name=f"h{b}{t}")
+            g = gain_sb[:, b, t : t + 1]
+            for half in range(2):
+                cols = slice(BANK * half, BANK * (half + 1))
+                nc.scalar.activation(bounded[:, cols], accs[half][:], ACT.Tanh, bias=bias_sb[:, b, t : t + 1])
+                if on_vector:
+                    nc.vector.tensor_scalar(h[:, cols], bounded[:, cols], g, None, ALU.mult)
+            if not on_vector:
+                nc.scalar.activation(h[:], bounded[:], ACT.Copy, scale=g)
+            return h
+
+        def pick(h, h1, h2, t):
+            nc.vector.tensor_copy(h1[:, t, :], h[:].indirect(pos1_sb[:]))
+            nc.vector.tensor_copy(h2[:, t, :], h[:].indirect(pos2_sb[:]))
+
+        def combine(h1, h2, m0, m1, name):
+            made = []
+            for op, kind in ((ALU.subtract, "diff"), (ALU.min, "low")):
+                grouped = keep.tile([P, (m1 - m0) * PACK], BF16, name=f"{kind}{name}", align_bytes=64)
+                nc.vector.tensor_tensor(
+                    grouped[:].rearrange("p (c i t) -> p c t i", i=4, t=PACK),
+                    h1[:, :, m0:m1].rearrange("p t (c i) -> p c t i", i=4),
+                    h2[:, :, m0:m1].rearrange("p t (c i) -> p c t i", i=4),
+                    op,
+                )
+                made.append((grouped, f"{kind}{name}"))
+            return [quantize(grouped, name) for grouped, name in made]
+
+        h1 = work.tile([P, PACK, PAIRS], F32, name="h1", tag="h1")
+        h2 = work.tile([P, PACK, PAIRS], F32, name="h2", tag="h2")
+        for t in range(PACK):
+            accs = [bank(2 * t + half) for half in range(2)]
+            for a in range(K_PASSES):
+                for half in range(2):
+                    first_pass(accs[half], a, 0, t, half)
+            pick(features(accs, 0, t, t < VECTOR_GAIN_SLICES), h1, h2, t)
+            if t < K_PASSES:
+                operand = quantize(round_w1(load_w1(t, 1), 0, PACK, nc.scalar.copy, "w1_all"), f"w1_{t}_1")
+                for u in range(PACK):
+                    w1q[t, 1, u] = columns(operand, P * u, P * (u + 1))
+
+        hs = []
+        for t in range(PACK):
+            accs = [bank(2 * t + half) for half in range(2)]
+            for a in range(K_PASSES):
+                for half in range(2):
+                    first_pass(accs[half], a, 1, t, half)
+            hs.append(features(accs, 1, t, False))
+        diff0, low0 = combine(h1, h2, 0, PAIRS, "0")
+
+        wm_grouped = keep.tile([P, H_PASSES, N * PACK], BF16, name="wm_grouped", align_bytes=64)
+        for b in range(H_PASSES):
+            raw = load_rows(wm[K_PASS * b : K_PASS * (b + 1), :])
+            nc.scalar.copy(
+                wm_grouped[:, b, :].rearrange("p (c i j) -> p c j i", i=4, j=PACK),
+                raw[:].rearrange("p j (c i) -> p c j i", i=4),
+            )
+        wd_codes = stage.tile([P, H_PASSES, 2 * N], U8, name="wd_codes", tag="raw", align_bytes=64)
+        nc.sync.dma_start(out=wd_codes[:].bitcast(I32), in_=wd_words.rearrange("b p c -> p b c").bitcast(I32))
+
+        h1 = work.tile([P, PACK, PAIRS], F32, name="h1", tag="h1")
+        h2 = work.tile([P, PACK, PAIRS], F32, name="h2", tag="h2")
+        for t in range(PACK):
+            pick(hs[t], h1, h2, t)
+
+        wm_codes = keep.tile([P, H_PASSES * N], U32, name="wm_codes", align_bytes=64)
+        wm_planes = keep.tile([P, H_PASSES * N], U8, name="wm_planes", align_bytes=64)
+        wm_flat = wm_grouped[:].rearrange("p b c -> p (b c)")
+        for c0, c1 in ((0, 512), (512, 768)):
+            nc.vector.quantize_mx(
+                out=wm_codes[:, c0:c1].bitcast(FP8X4), scales=wm_planes[:, c0:c1], in_=wm_flat[:, PACK * c0 : PACK * c1]
+            )
+
+        def second_passes(acc_diff, acc_low, b, diff, low):
+            for u in range(N_SLICES):
+                nc.tensor.matmul_mx(
+                    out=acc_diff[:, P * u : P * (u + 1)],
+                    lhsT=wd_codes[:, b, 2 * P * u : 2 * P * (u + 1)].bitcast(FP4X4),
+                    lhsT_scale=wd_planes[:, b, P * u : P * (u + 1)],
+                    rhs=diff[0].bitcast(FP8X4),
+                    rhs_scale=diff[1],
+                    start=(b == 0 and u == 0),
+                    stop=(b == H_PASSES - 1 and u == N_SLICES - 1),
+                )
+            for u in range(N_SLICES):
+                cols = slice(N * b + P * u, N * b + P * (u + 1))
+                nc.tensor.matmul_mx(
+                    out=acc_low[:, P * u : P * (u + 1)],
+                    lhsT=wm_codes[:, cols].bitcast(FP8X4),
+                    lhsT_scale=wm_planes[:, cols],
+                    rhs=low[0].bitcast(FP8X4),
+                    rhs_scale=low[1],
+                    start=(b == 0 and u == 0),
+                    stop=(b == H_PASSES - 1 and u == N_SLICES - 1),
+                )
+
+        chunks = PAIRS // CHUNK
+        sums = [(bank(2 * q), bank(2 * q + 1)) for q in range(chunks)]
+        for q in range(chunks):
+            c0, c1 = CHUNK * q, CHUNK * (q + 1)
+            second_passes(*sums[q], 0, columns(diff0, c0, c1), columns(low0, c0, c1))
+
+        out_view = out.rearrange("(u p) m -> p u m", p=P)
+        for m0, m1 in ((0, 256), (256, 384), (384, 512)):
+            diff1, low1 = combine(h1, h2, m0, m1, f"1_{m0}")
+            for q in range(m0 // CHUNK, m1 // CHUNK):
+                c0, c1 = CHUNK * q - m0, CHUNK * (q + 1) - m0
+                second_passes(*sums[q], 1, columns(diff1, c0, c1), columns(low1, c0, c1))
+                size = work.tile([P, N], F32, name="size", tag="size")
+                nc.scalar.activation(size[:], sums[q][0][:, :N], ACT.Abs)
+                logs = work.tile([P, N], F32, name="logs", tag="logs")
+                nc.scalar.activation(logs[:], size[:], ACT.Ln, bias=1.0)
+                scores = keep.tile([P, N], F32, name=f"scores{q}")
+                nc.vector.tensor_tensor(scores[:], sums[q][1][:, :N], logs[:], ALU.add)
+                nc.sync.dma_start(
+                    out=out_view[:, :, CHUNK * q : CHUNK * (q + 1)],
+                    in_=scores[:].rearrange("p (u m) -> p u m", m=CHUNK),
+                )

@@ -24,7 +24,6 @@ H_PASSES = H // K_PASS
 BANK = 512
 N_SLICES = N // P
 CHUNK = 128
-VECTOR_GAIN_SLICES = 2
 
 
 def tile_list_deed_defect_scores_kernel(
@@ -33,7 +32,7 @@ def tile_list_deed_defect_scores_kernel(
     nc = tc.nc
     with ExitStack() as ctx:
         keep = ctx.enter_context(tc.tile_pool(name="keep", bufs=1))
-        stage = ctx.enter_context(tc.tile_pool(name="stage", bufs=5))
+        stage = ctx.enter_context(tc.tile_pool(name="stage", bufs=3))
         work = ctx.enter_context(tc.tile_pool(name="work", bufs=2))
         psum = ctx.enter_context(tc.psum_pool(name="psum", bufs=1))
 
@@ -44,19 +43,19 @@ def tile_list_deed_defect_scores_kernel(
         nc.sync.dma_start(offs_sb[:], offs)
         nc.sync.dma_start(pos1_sb[:], pos1)
         nc.sync.dma_start(pos2_sb[:], pos2)
-        scale_window = stage.tile([P, T], U8, name="scale_window", tag="raw", align_bytes=64)
+        scale_window = keep.tile([P, T], U8, name="scale_window", tag="picked0", align_bytes=64)
         nc.vector.memset(scale_window[:].bitcast(I32), 0)
         for a in range(K_PASSES):
             rows = tab_scales[a].bitcast(I32).rearrange("(g e) c -> e g c", e=2)
             for e in range(2):
                 nc.scalar.dma_start(out=scale_window[4 * a + e : P : 16, :].bitcast(I32), in_=rows[e])
         warm_in = stage.tile([P, 1], F32, name="warm_in", tag="raw", align_bytes=64)
-        warm_out = stage.tile([P, 1], F32, name="warm_out", tag="raw", align_bytes=64)
+        warm_out = keep.tile([P, 1], F32, name="warm_out", tag="last_table", align_bytes=64)
         nc.vector.memset(warm_in[:], 0.0)
         nc.scalar.activation(warm_out[:], warm_in[:], ACT.Tanh)
 
-        def load_table(a):
-            words = stage.tile([P, T], U32, name="words", tag="raw", align_bytes=64)
+        def load_table(a, pool, tag):
+            words = pool.tile([P, T], U32, name="words", tag=tag, align_bytes=64)
             nc.sync.dma_start(
                 out=words[:].bitcast(I32), in_=tab_words[a].rearrange("p t i -> p (t i)").bitcast(I32)
             )
@@ -70,46 +69,42 @@ def tile_list_deed_defect_scores_kernel(
         def load_w1(a, b):
             return load_rows(w1[K_PASS * a : K_PASS * (a + 1), K_PASS * b : K_PASS * (b + 1)])
 
-        tables = [load_table(0), load_table(1)]
+        tables = [load_table(0, stage, "raw")]
+        raw_first = load_w1(0, 0)
+        tables.append(load_table(1, stage, "raw"))
+        tables.append(load_table(2, keep, "last_table"))
+        vectors = keep.tile([P, 2, H_PASSES, PACK], F32, name="vectors")
+        bias_sb, gain_sb = vectors[:, 0], vectors[:, 1]
+        nc.gpsimd.dma_start(out=bias_sb, in_=b1.rearrange("(b p t) -> p b t", p=P, t=PACK))
+        nc.gpsimd.dma_start(out=gain_sb, in_=gain.rearrange("(b p t) -> p b t", p=P, t=PACK))
 
-        bias_sb = keep.tile([P, H_PASSES, PACK], F32, name="bias_sb")
-        gain_sb = keep.tile([P, H_PASSES, PACK], F32, name="gain_sb")
-        nc.gpsimd.dma_start(out=bias_sb[:], in_=b1.rearrange("(b p t) -> p b t", p=P, t=PACK))
-        nc.gpsimd.dma_start(out=gain_sb[:], in_=gain.rearrange("(b p t) -> p b t", p=P, t=PACK))
-        wd_planes = keep.tile([P, H_PASSES, N], U8, name="wd_planes", align_bytes=64)
-        nc.gpsimd.memset(wd_planes[:].bitcast(I32), 0)
-        for d in range(4):
-            nc.gpsimd.dma_start(
-                out=wd_planes[32 * d : 32 * d + 4].bitcast(I32),
-                in_=wd_scales[:, 4 * d : 4 * d + 4, :].rearrange("b r c -> r b c").bitcast(I32),
-            )
 
         picked_scales = keep.tile([P, S], U8, name="picked_scales", align_bytes=64)
         nc.vector.tensor_copy(picked_scales[:], scale_window[:].indirect(offs_sb[:]))
         table_planes = keep.tile([P, S], U8, name="table_planes", align_bytes=64)
         nc.vector.tensor_copy(table_planes[:].bitcast(I32), picked_scales[:].bitcast(I32))
         for e in range(2):
-            nc.scalar.dma_start(
+            nc.sync.dma_start(
                 out=table_planes[2 + e : P - 16 : 4, :].bitcast(I32),
                 in_=picked_scales[16 + e : P : 4, :].bitcast(I32),
             )
 
         def gather_table(a):
-            picked = keep.tile([P, S], U32, name=f"picked{a}", align_bytes=64)
+            picked = keep.tile([P, S], U32, name=f"picked{a}", tag=f"picked{a}", align_bytes=64)
             nc.vector.tensor_copy(picked[:], tables[a][:].indirect(offs_sb[:]))
             return picked
 
-        def round_w1(raw, t0, t1, copy, name):
-            grouped = work.tile([P, (t1 - t0) * K_PASS], BF16, name=name, tag=name, align_bytes=64)
+        def round_w1(raw, t0, t1, copy, tag, pool=work):
+            grouped = pool.tile([P, (t1 - t0) * K_PASS], BF16, name="grouped", tag=tag, align_bytes=64)
             copy(
                 grouped[:].rearrange("p (t m j) -> p m j t", m=P, j=PACK),
                 raw[:].rearrange("p j (m t) -> p m j t", t=PACK)[:, :, :, t0:t1],
             )
             return grouped
 
-        def quantize(grouped, name):
+        def quantize(grouped, name, tag=None):
             width = grouped.shape[1] // PACK
-            codes = keep.tile([P, width], U32, name=name + "_codes", align_bytes=64)
+            codes = keep.tile([P, width], U32, name=name + "_codes", tag=tag or name + "_codes", align_bytes=64)
             scales = keep.tile([P, width], U8, name=name + "_scales", align_bytes=64)
             nc.vector.quantize_mx(out=codes[:].bitcast(FP8X4), scales=scales[:], in_=grouped[:])
             return codes, scales
@@ -119,20 +114,25 @@ def tile_list_deed_defect_scores_kernel(
 
         w1q = {}
 
-        def split_w1(a, raw):
-            low_half = round_w1(raw, 0, 2, nc.vector.tensor_copy, "w1_v")
-            high_half = round_w1(raw, 2, 4, nc.scalar.copy, "w1_s")
-            for t0, half in ((0, low_half), (2, high_half)):
-                operand = quantize(half, f"w1_{a}_0_{t0}")
-                for t in range(2):
-                    w1q[a, 0, t0 + t] = columns(operand, P * t, P * (t + 1))
+        def quantize_w1(a, b, t0, grouped, tag=None):
+            operand = quantize(grouped, f"w1_{a}_{b}_{t0}", tag)
+            for u in range(grouped.shape[1] // K_PASS):
+                w1q[a, b, t0 + u] = columns(operand, P * u, P * (u + 1))
 
-        picked = [gather_table(0), gather_table(1)]
-        split_w1(0, load_w1(0, 0))
-        tables.append(load_table(2))
-        picked.append(gather_table(2))
-        split_w1(1, load_w1(1, 0))
-        split_w1(2, load_w1(2, 0))
+        def whole_w1(a, b, raw, tag):
+            quantize_w1(a, b, 0, round_w1(raw, 0, PACK, nc.scalar.copy, tag))
+
+        picked = [gather_table(0)]
+        for t0, tag in ((0, "picked1"), (2, "picked2")):
+            quantize_w1(0, 0, t0, round_w1(raw_first, t0, t0 + 2, nc.scalar.copy, tag, keep))
+        picked += [gather_table(1), gather_table(2)]
+        raw = load_w1(1, 0)
+        halves = [round_w1(raw, t0, t0 + 2, nc.scalar.copy, "w1_s") for t0 in (0, 2)]
+        quantize_w1(1, 0, 0, halves[0], "last_table")
+        raw = load_w1(2, 0)
+        quantize_w1(2, 0, 0, round_w1(raw, 0, 2, nc.vector.tensor_copy, "last_low", keep))
+        quantize_w1(1, 0, 2, halves[1], "last_low")
+        quantize_w1(2, 0, 2, round_w1(raw, 2, 4, nc.vector.tensor_copy, "w1_v"))
 
         def bank(i):
             return psum.tile([P, BANK], F32, name=f"bank{i}", tag=f"bank{i}")
@@ -149,48 +149,51 @@ def tile_list_deed_defect_scores_kernel(
                 stop=(a == K_PASSES - 1),
             )
 
-        def features(accs, b, t, on_vector):
-            bounded = work.tile([P, S], F32, name="bounded", tag="bounded")
+        def features(accs, b, t, on_vector, tag="bounded"):
+            bounded = work.tile([P, S], F32, name="bounded", tag=tag, align_bytes=64)
             h = keep.tile([P, S], F32, name=f"h{b}{t}")
             g = gain_sb[:, b, t : t + 1]
             for half in range(2):
                 cols = slice(BANK * half, BANK * (half + 1))
                 nc.scalar.activation(bounded[:, cols], accs[half][:], ACT.Tanh, bias=bias_sb[:, b, t : t + 1])
-                if on_vector:
+                if (b, t) == (0, 0):
                     nc.vector.tensor_scalar(h[:, cols], bounded[:, cols], g, None, ALU.mult)
+            if on_vector and (b, t) != (0, 0):
+                nc.vector.tensor_scalar(h[:], bounded[:], g, None, ALU.mult)
             if not on_vector:
                 nc.scalar.activation(h[:], bounded[:], ACT.Copy, scale=g)
+            if (b, t) == (H_PASSES - 1, PACK - 1):
+                warm_log = keep.tile([P, 1], F32, name="warm_log")
+                nc.scalar.activation(warm_log[:], bounded[:, 0:1], ACT.Ln, bias=1.0, scale=0.0)
             return h
 
         def pick(h, h1, h2, t):
             nc.vector.tensor_copy(h1[:, t, :], h[:].indirect(pos1_sb[:]))
             nc.vector.tensor_copy(h2[:, t, :], h[:].indirect(pos2_sb[:]))
 
-        def combine(h1, h2, m0, m1, name):
-            made = []
-            for op, kind in ((ALU.subtract, "diff"), (ALU.min, "low")):
-                grouped = keep.tile([P, (m1 - m0) * PACK], BF16, name=f"{kind}{name}", align_bytes=64)
-                nc.vector.tensor_tensor(
-                    grouped[:].rearrange("p (c i t) -> p c t i", i=4, t=PACK),
-                    h1[:, :, m0:m1].rearrange("p t (c i) -> p c t i", i=4),
-                    h2[:, :, m0:m1].rearrange("p t (c i) -> p c t i", i=4),
-                    op,
-                )
-                made.append((grouped, f"{kind}{name}"))
-            return [quantize(grouped, name) for grouped, name in made]
+        def combine(op, h1, h2, m0, m1, pool, tag):
+            grouped = pool.tile([P, (m1 - m0) * PACK], BF16, name="grouped", tag=tag, align_bytes=64)
+            nc.vector.tensor_tensor(
+                grouped[:].rearrange("p (c i t) -> p c t i", i=4, t=PACK),
+                h1[:, :, m0:m1].rearrange("p t (c i) -> p c t i", i=4),
+                h2[:, :, m0:m1].rearrange("p t (c i) -> p c t i", i=4),
+                op,
+            )
+            return grouped
 
         h1 = work.tile([P, PACK, PAIRS], F32, name="h1", tag="h1")
         h2 = work.tile([P, PACK, PAIRS], F32, name="h2", tag="h2")
-        for t in range(PACK):
-            accs = [bank(2 * t + half) for half in range(2)]
-            for a in range(K_PASSES):
-                for half in range(2):
-                    first_pass(accs[half], a, 0, t, half)
-            pick(features(accs, 0, t, t < VECTOR_GAIN_SLICES), h1, h2, t)
-            if t < K_PASSES:
-                operand = quantize(round_w1(load_w1(t, 1), 0, PACK, nc.scalar.copy, "w1_all"), f"w1_{t}_1")
-                for u in range(PACK):
-                    w1q[t, 1, u] = columns(operand, P * u, P * (u + 1))
+        accs = [[bank(2 * t + half) for half in range(2)] for t in range(PACK)]
+        for a, t in [(0, 0), (0, 1), (0, 2), (0, 3), (1, 0), (1, 1), (2, 0), (2, 1), (1, 2), (2, 2), (1, 3), (2, 3)]:
+            for half in range(2):
+                first_pass(accs[t][half], a, 0, t, half)
+        for t in range(2):
+            pick(features(accs[t], 0, t, True, "turns"), h1, h2, t)
+        whole_w1(0, 1, load_w1(0, 1), "turns")
+        for t in range(2, PACK):
+            pick(features(accs[t], 0, t, t == 2), h1, h2, t)
+        for a in range(1, K_PASSES):
+            whole_w1(a, 1, load_w1(a, 1), "turns")
 
         hs = []
         for t in range(PACK):
@@ -199,7 +202,8 @@ def tile_list_deed_defect_scores_kernel(
                 for half in range(2):
                     first_pass(accs[half], a, 1, t, half)
             hs.append(features(accs, 1, t, False))
-        diff0, low0 = combine(h1, h2, 0, PAIRS, "0")
+        diff0, low0 = [combine(op, h1, h2, 0, PAIRS, work, "turns") for op in (ALU.subtract, ALU.min)]
+        diff0, low0 = quantize(diff0, "diff0"), quantize(low0, "low0")
 
         wm_grouped = keep.tile([P, H_PASSES, N * PACK], BF16, name="wm_grouped", align_bytes=64)
         for b in range(H_PASSES):
@@ -210,6 +214,13 @@ def tile_list_deed_defect_scores_kernel(
             )
         wd_codes = stage.tile([P, H_PASSES, 2 * N], U8, name="wd_codes", tag="raw", align_bytes=64)
         nc.sync.dma_start(out=wd_codes[:].bitcast(I32), in_=wd_words.rearrange("b p c -> p b c").bitcast(I32))
+        wd_planes = stage.tile([P, H_PASSES, N], U8, name="wd_planes", tag="raw", align_bytes=64)
+        nc.gpsimd.memset(wd_planes[:].bitcast(I32), 0)
+        for d in range(4):
+            nc.sync.dma_start(
+                out=wd_planes[32 * d : 32 * d + 4].bitcast(I32),
+                in_=wd_scales[:, 4 * d : 4 * d + 4, :].rearrange("b r c -> r b c").bitcast(I32),
+            )
 
         h1 = work.tile([P, PACK, PAIRS], F32, name="h1", tag="h1")
         h2 = work.tile([P, PACK, PAIRS], F32, name="h2", tag="h2")
@@ -224,7 +235,7 @@ def tile_list_deed_defect_scores_kernel(
                 out=wm_codes[:, c0:c1].bitcast(FP8X4), scales=wm_planes[:, c0:c1], in_=wm_flat[:, PACK * c0 : PACK * c1]
             )
 
-        def second_passes(acc_diff, acc_low, b, diff, low):
+        def diff_passes(acc_diff, b, diff):
             for u in range(N_SLICES):
                 nc.tensor.matmul_mx(
                     out=acc_diff[:, P * u : P * (u + 1)],
@@ -235,6 +246,8 @@ def tile_list_deed_defect_scores_kernel(
                     start=(b == 0 and u == 0),
                     stop=(b == H_PASSES - 1 and u == N_SLICES - 1),
                 )
+
+        def low_passes(acc_low, b, low):
             for u in range(N_SLICES):
                 cols = slice(N * b + P * u, N * b + P * (u + 1))
                 nc.tensor.matmul_mx(
@@ -251,21 +264,46 @@ def tile_list_deed_defect_scores_kernel(
         sums = [(bank(2 * q), bank(2 * q + 1)) for q in range(chunks)]
         for q in range(chunks):
             c0, c1 = CHUNK * q, CHUNK * (q + 1)
-            second_passes(*sums[q], 0, columns(diff0, c0, c1), columns(low0, c0, c1))
+            diff_passes(sums[q][0], 0, columns(diff0, c0, c1))
+            low_passes(sums[q][1], 0, columns(low0, c0, c1))
 
         out_view = out.rearrange("(u p) m -> p u m", p=P)
-        for m0, m1 in ((0, 256), (256, 384), (384, 512)):
-            diff1, low1 = combine(h1, h2, m0, m1, f"1_{m0}")
-            for q in range(m0 // CHUNK, m1 // CHUNK):
-                c0, c1 = CHUNK * q - m0, CHUNK * (q + 1) - m0
-                second_passes(*sums[q], 1, columns(diff1, c0, c1), columns(low1, c0, c1))
+        logs = {}
+
+        def finish_diff(grouped, q0, q1):
+            diff = quantize(grouped, f"diff1_{q0}")
+            for q in range(q0, q1):
+                diff_passes(sums[q][0], 1, columns(diff, CHUNK * (q - q0), CHUNK * (q - q0 + 1)))
                 size = work.tile([P, N], F32, name="size", tag="size")
                 nc.scalar.activation(size[:], sums[q][0][:, :N], ACT.Abs)
-                logs = work.tile([P, N], F32, name="logs", tag="logs")
-                nc.scalar.activation(logs[:], size[:], ACT.Ln, bias=1.0)
-                scores = keep.tile([P, N], F32, name=f"scores{q}")
-                nc.vector.tensor_tensor(scores[:], sums[q][1][:, :N], logs[:], ALU.add)
-                nc.sync.dma_start(
-                    out=out_view[:, :, CHUNK * q : CHUNK * (q + 1)],
-                    in_=scores[:].rearrange("p (u m) -> p u m", m=CHUNK),
-                )
+                logs[q] = keep.tile([P, N], F32, name=f"logs{q}")
+                nc.scalar.activation(logs[q][:], size[:], ACT.Ln, bias=1.0)
+
+        def finish_low(grouped, q0, q1):
+            low = quantize(grouped, f"low1_{q0}")
+            for q in range(q0, q1):
+                low_passes(sums[q][1], 1, columns(low, CHUNK * (q - q0), CHUNK * (q - q0 + 1)))
+
+        def pairs(op, q0, q1):
+            return combine(op, h1, h2, CHUNK * q0, CHUNK * q1, keep, f"pairs{q0}_{op == ALU.min}")
+
+        def store(q):
+            scores = keep.tile([P, N], F32, name=f"scores{q}")
+            nc.vector.tensor_tensor(scores[:], sums[q][1][:, :N], logs[q][:], ALU.add)
+            nc.sync.dma_start(
+                out=out_view[:, :, CHUNK * q : CHUNK * (q + 1)],
+                in_=scores[:].rearrange("p (u m) -> p u m", m=CHUNK),
+            )
+
+        for q0, q1 in ((0, 2), (2, 3)):
+            diff, low = pairs(ALU.subtract, q0, q1), pairs(ALU.min, q0, q1)
+            finish_diff(diff, q0, q1)
+            finish_low(low, q0, q1)
+        store(0)
+        diff = pairs(ALU.subtract, 3, 4)
+        store(1)
+        finish_diff(diff, 3, 4)
+        low = pairs(ALU.min, 3, 4)
+        store(2)
+        finish_low(low, 3, 4)
+        store(3)

@@ -119,8 +119,17 @@ def tile_list_deed_defect_scores_kernel(
             for u in range(grouped.shape[1] // K_PASS):
                 w1q[a, b, t0 + u] = columns(operand, P * u, P * (u + 1))
 
-        def whole_w1(a, b, raw, tag):
-            quantize_w1(a, b, 0, round_w1(raw, 0, PACK, nc.scalar.copy, tag))
+        def round_w1_on_gpsimd(raw, tag):
+            grouped = keep.tile([P, PACK * K_PASS], BF16, name="grouped", tag=tag, align_bytes=64)
+            nc.gpsimd.tensor_scalar(
+                grouped[:].rearrange("p (t m j) -> p m t j", m=P, j=PACK),
+                raw[:].rearrange("p j (m t) -> p m t j", t=PACK),
+                1.0,
+                0.0,
+                ALU.mult,
+                ALU.add,
+            )
+            return grouped
 
         picked = [gather_table(0)]
         for t0, tag in ((0, "picked1"), (2, "picked2")):
@@ -149,18 +158,16 @@ def tile_list_deed_defect_scores_kernel(
                 stop=(a == K_PASSES - 1),
             )
 
-        def features(accs, b, t, on_vector, tag="bounded"):
-            bounded = work.tile([P, S], F32, name="bounded", tag=tag, align_bytes=64)
-            h = keep.tile([P, S], F32, name=f"h{b}{t}")
+        def features(accs, b, t, pool=work, tag="bounded"):
+            bounded = pool.tile([P, S], F32, name="bounded", tag=tag, align_bytes=64)
+            h = keep.tile([P, S], F32, name=f"h{b}{t}", tag=f"h{b}{t}", align_bytes=64)
             g = gain_sb[:, b, t : t + 1]
             for half in range(2):
                 cols = slice(BANK * half, BANK * (half + 1))
                 nc.scalar.activation(bounded[:, cols], accs[half][:], ACT.Tanh, bias=bias_sb[:, b, t : t + 1])
                 if (b, t) == (0, 0):
                     nc.vector.tensor_scalar(h[:, cols], bounded[:, cols], g, None, ALU.mult)
-            if on_vector and (b, t) != (0, 0):
-                nc.vector.tensor_scalar(h[:], bounded[:], g, None, ALU.mult)
-            if not on_vector:
+            if (b, t) != (0, 0):
                 nc.scalar.activation(h[:], bounded[:], ACT.Copy, scale=g)
             if (b, t) == (H_PASSES - 1, PACK - 1):
                 warm_log = keep.tile([P, 1], F32, name="warm_log")
@@ -171,9 +178,9 @@ def tile_list_deed_defect_scores_kernel(
             nc.vector.tensor_copy(h1[:, t, :], h[:].indirect(pos1_sb[:]))
             nc.vector.tensor_copy(h2[:, t, :], h[:].indirect(pos2_sb[:]))
 
-        def combine(op, h1, h2, m0, m1, pool, tag):
+        def combine(op, h1, h2, m0, m1, pool, tag, engine=nc.vector):
             grouped = pool.tile([P, (m1 - m0) * PACK], BF16, name="grouped", tag=tag, align_bytes=64)
-            nc.vector.tensor_tensor(
+            engine.tensor_tensor(
                 grouped[:].rearrange("p (c i t) -> p c t i", i=4, t=PACK),
                 h1[:, :, m0:m1].rearrange("p t (c i) -> p c t i", i=4),
                 h2[:, :, m0:m1].rearrange("p t (c i) -> p c t i", i=4),
@@ -187,13 +194,15 @@ def tile_list_deed_defect_scores_kernel(
         for a, t in [(0, 0), (0, 1), (0, 2), (0, 3), (1, 0), (1, 1), (2, 0), (2, 1), (1, 2), (2, 2), (1, 3), (2, 3)]:
             for half in range(2):
                 first_pass(accs[t][half], a, 0, t, half)
+        rounded = []
         for t in range(2):
-            pick(features(accs[t], 0, t, True, "turns"), h1, h2, t)
-        whole_w1(0, 1, load_w1(0, 1), "turns")
-        for t in range(2, PACK):
-            pick(features(accs[t], 0, t, t == 2), h1, h2, t)
-        for a in range(1, K_PASSES):
-            whole_w1(a, 1, load_w1(a, 1), "turns")
+            pick(features(accs[t], 0, t, keep, f"gate{t}"), h1, h2, t)
+            rounded.append(round_w1_on_gpsimd(load_w1(t, 1), f"gate{t}"))
+        pick(features(accs[2], 0, 2), h1, h2, 2)
+        quantize_w1(0, 1, 0, rounded[0], "h02")
+        quantize_w1(1, 1, 0, rounded[1])
+        pick(features(accs[3], 0, 3), h1, h2, 3)
+        quantize_w1(2, 1, 0, round_w1(load_w1(2, 1), 0, PACK, nc.scalar.copy, "chain", keep))
 
         hs = []
         for t in range(PACK):
@@ -201,9 +210,9 @@ def tile_list_deed_defect_scores_kernel(
             for a in range(K_PASSES):
                 for half in range(2):
                     first_pass(accs[half], a, 1, t, half)
-            hs.append(features(accs, 1, t, False))
-        diff0, low0 = [combine(op, h1, h2, 0, PAIRS, work, "turns") for op in (ALU.subtract, ALU.min)]
-        diff0, low0 = quantize(diff0, "diff0"), quantize(low0, "low0")
+            hs.append(features(accs, 1, t))
+        low0 = quantize(combine(ALU.min, h1, h2, 0, PAIRS, keep, "chain"), "low0")
+        diff0 = combine(ALU.subtract, h1, h2, 0, PAIRS, keep, "chain", nc.gpsimd)
 
         wm_grouped = keep.tile([P, H_PASSES, N * PACK], BF16, name="wm_grouped", align_bytes=64)
         for b in range(H_PASSES):
@@ -226,8 +235,10 @@ def tile_list_deed_defect_scores_kernel(
         h2 = work.tile([P, PACK, PAIRS], F32, name="h2", tag="h2")
         for t in range(PACK):
             pick(hs[t], h1, h2, t)
+            if t == 2:
+                diff0 = quantize(diff0, "diff0", "h12")
 
-        wm_codes = keep.tile([P, H_PASSES * N], U32, name="wm_codes", align_bytes=64)
+        wm_codes = keep.tile([P, H_PASSES * N], U32, name="wm_codes", tag="chain", align_bytes=64)
         wm_planes = keep.tile([P, H_PASSES * N], U8, name="wm_planes", align_bytes=64)
         wm_flat = wm_grouped[:].rearrange("p b c -> p (b c)")
         for c0, c1 in ((0, 512), (512, 768)):

from contextlib import ExitStack

import concourse.mybir as mybir

K, T, S, H, PAIRS, N = 1536, 2048, 1024, 1024, 512, 384
FLOPS = 2 * K * H * S + 2 * 2 * H * N * PAIRS

F32 = mybir.dt.float32
BF16 = mybir.dt.bfloat16
I32 = mybir.dt.int32
U32 = mybir.dt.uint32
U16 = mybir.dt.uint16
U8 = mybir.dt.uint8
FP8X4 = mybir.dt.float8_e4m3fn_x4
FP4X4 = mybir.dt.float4_e2m1fn_x4
ALU = mybir.AluOpType
ACT = mybir.ActivationFunctionType

P = 128
PACK = 4
K_PASS = P * PACK
K_PASSES = K // K_PASS
H_PASSES = H // K_PASS
BANK = 512
N_SLICES = N // P
CHUNK = 128


def tile_list_deed_defect_scores_kernel(
    tc, tab_words, tab_scales, offs, pos1, pos2, w1, b1, gain, wd_words, wd_scales, wm, out
):
    nc = tc.nc
    with ExitStack() as ctx:
        keep = ctx.enter_context(tc.tile_pool(name="keep", bufs=1))
        stage = ctx.enter_context(tc.tile_pool(name="stage", bufs=3))
        work = ctx.enter_context(tc.tile_pool(name="work", bufs=2))
        psum = ctx.enter_context(tc.psum_pool(name="psum", bufs=1))

        offs_sb = keep.tile([P, S // 16], U16, name="offs_sb")
        pos1_sb = keep.tile([P, PAIRS // 16], U16, name="pos1_sb")
        pos2_sb = keep.tile([P, PAIRS // 16], U16, name="pos2_sb")

        nc.sync.dma_start(offs_sb[:], offs)
        nc.sync.dma_start(pos1_sb[:], pos1)
        nc.sync.dma_start(pos2_sb[:], pos2)
        scale_window = keep.tile([P, T], U8, name="scale_window", tag="picked0", align_bytes=64)
        nc.vector.memset(scale_window[:].bitcast(I32), 0)
        for a in range(K_PASSES):
            rows = tab_scales[a].bitcast(I32).rearrange("(g e) c -> e g c", e=2)
            for e in range(2):
                nc.scalar.dma_start(out=scale_window[4 * a + e : P : 16, :].bitcast(I32), in_=rows[e])
        warm_in = stage.tile([P, 1], F32, name="warm_in", tag="raw", align_bytes=64)
        warm_out = keep.tile([P, 1], F32, name="warm_out", tag="last_table", align_bytes=64)
        nc.vector.memset(warm_in[:], 0.0)
        nc.scalar.activation(warm_out[:], warm_in[:], ACT.Tanh)

        def load_table(a, pool, tag):
            words = pool.tile([P, T], U32, name="words", tag=tag, align_bytes=64)
            nc.sync.dma_start(
                out=words[:].bitcast(I32), in_=tab_words[a].rearrange("p t i -> p (t i)").bitcast(I32)
            )
            return words

        def load_rows(src):
            raw = stage.tile([P, PACK, src.shape[1]], F32, name="raw", tag="raw", align_bytes=64)
            nc.sync.dma_start(out=raw[:], in_=src.rearrange("(p j) c -> p j c", j=PACK))
            return raw

        def load_w1(a, b):
            return load_rows(w1[K_PASS * a : K_PASS * (a + 1), K_PASS * b : K_PASS * (b + 1)])

        tables = [load_table(0, stage, "raw")]
        raw_first = load_w1(0, 0)
        tables.append(load_table(1, stage, "raw"))
        tables.append(load_table(2, keep, "last_table"))
        vectors = keep.tile([P, 2, H_PASSES, PACK], F32, name="vectors")
        bias_sb, gain_sb = vectors[:, 0], vectors[:, 1]
        nc.gpsimd.dma_start(out=bias_sb, in_=b1.rearrange("(b p t) -> p b t", p=P, t=PACK))
        nc.gpsimd.dma_start(out=gain_sb, in_=gain.rearrange("(b p t) -> p b t", p=P, t=PACK))


        picked_scales = keep.tile([P, S], U8, name="picked_scales", align_bytes=64)
        nc.vector.tensor_copy(picked_scales[:], scale_window[:].indirect(offs_sb[:]))
        table_planes = keep.tile([P, S], U8, name="table_planes", align_bytes=64)
        nc.vector.tensor_copy(table_planes[:].bitcast(I32), picked_scales[:].bitcast(I32))
        for e in range(2):
            nc.sync.dma_start(
                out=table_planes[2 + e : P - 16 : 4, :].bitcast(I32),
                in_=picked_scales[16 + e : P : 4, :].bitcast(I32),
            )

        def gather_table(a):
            picked = keep.tile([P, S], U32, name=f"picked{a}", tag=f"picked{a}", align_bytes=64)
            nc.vector.tensor_copy(picked[:], tables[a][:].indirect(offs_sb[:]))
            return picked

        def round_w1(raw, t0, t1, copy, tag, pool=work):
            grouped = pool.tile([P, (t1 - t0) * K_PASS], BF16, name="grouped", tag=tag, align_bytes=64)
            copy(
                grouped[:].rearrange("p (t m j) -> p m j t", m=P, j=PACK),
                raw[:].rearrange("p j (m t) -> p m j t", t=PACK)[:, :, :, t0:t1],
            )
            return grouped

        def quantize(grouped, name, tag=None):
            width = grouped.shape[1] // PACK
            codes = keep.tile([P, width], U32, name=name + "_codes", tag=tag or name + "_codes", align_bytes=64)
            scales = keep.tile([P, width], U8, name=name + "_scales", align_bytes=64)
            nc.vector.quantize_mx(out=codes[:].bitcast(FP8X4), scales=scales[:], in_=grouped[:])
            return codes, scales

        def columns(operand, c0, c1):
            return operand[0][:, c0:c1], operand[1][:, c0:c1]

        w1q = {}

        def quantize_w1(a, b, t0, grouped, tag=None):
            operand = quantize(grouped, f"w1_{a}_{b}_{t0}", tag)
            for u in range(grouped.shape[1] // K_PASS):
                w1q[a, b, t0 + u] = columns(operand, P * u, P * (u + 1))

        def round_w1_on_gpsimd(raw, tag):
            grouped = keep.tile([P, PACK * K_PASS], BF16, name="grouped", tag=tag, align_bytes=64)
            nc.gpsimd.tensor_scalar(
                grouped[:].rearrange("p (t m j) -> p m t j", m=P, j=PACK),
                raw[:].rearrange("p j (m t) -> p m t j", t=PACK),
                1.0,
                0.0,
                ALU.mult,
                ALU.add,
            )
            return grouped

        picked = [gather_table(0)]
        for t0, tag in ((0, "picked1"), (2, "picked2")):
            quantize_w1(0, 0, t0, round_w1(raw_first, t0, t0 + 2, nc.scalar.copy, tag, keep))
        picked += [gather_table(1), gather_table(2)]
        raw = load_w1(1, 0)
        halves = [round_w1(raw, t0, t0 + 2, nc.scalar.copy, "w1_s") for t0 in (0, 2)]
        quantize_w1(1, 0, 0, halves[0], "last_table")
        raw = load_w1(2, 0)
        quantize_w1(2, 0, 0, round_w1(raw, 0, 2, nc.vector.tensor_copy, "last_low", keep))
        quantize_w1(1, 0, 2, halves[1], "last_low")
        quantize_w1(2, 0, 2, round_w1(raw, 2, 4, nc.vector.tensor_copy, "w1_v"))

        def bank(i):
            return psum.tile([P, BANK], F32, name=f"bank{i}", tag=f"bank{i}")

        def first_pass(acc, a, b, t, half):
            cols = slice(BANK * half, BANK * (half + 1))
            nc.tensor.matmul_mx(
                out=acc[:],
                lhsT=w1q[a, b, t][0].bitcast(FP8X4),
                lhsT_scale=w1q[a, b, t][1],
                rhs=picked[a][:, cols].bitcast(FP8X4),
                rhs_scale=table_planes[4 * a : P, cols],
                start=(a == 0),
                stop=(a == K_PASSES - 1),
            )

        def features(accs, b, t, pool=work, tag="bounded"):
            bounded = pool.tile([P, S], F32, name="bounded", tag=tag, align_bytes=64)
            h = keep.tile([P, S], F32, name=f"h{b}{t}", tag=f"h{b}{t}", align_bytes=64)
            g = gain_sb[:, b, t : t + 1]
            for half in range(2):
                cols = slice(BANK * half, BANK * (half + 1))
                nc.scalar.activation(bounded[:, cols], accs[half][:], ACT.Tanh, bias=bias_sb[:, b, t : t + 1])
                if (b, t) == (0, 0):
                    nc.vector.tensor_scalar(h[:, cols], bounded[:, cols], g, None, ALU.mult)
            if (b, t) != (0, 0):
                nc.scalar.activation(h[:], bounded[:], ACT.Copy, scale=g)
            if (b, t) == (H_PASSES - 1, PACK - 1):
                warm_log = keep.tile([P, 1], F32, name="warm_log")
                nc.scalar.activation(warm_log[:], bounded[:, 0:1], ACT.Ln, bias=1.0, scale=0.0)
            return h

        def pick(h, h1, h2, t):
            nc.vector.tensor_copy(h1[:, t, :], h[:].indirect(pos1_sb[:]))
            nc.vector.tensor_copy(h2[:, t, :], h[:].indirect(pos2_sb[:]))

        def combine(op, h1, h2, m0, m1, pool, tag, engine=nc.vector):
            grouped = pool.tile([P, (m1 - m0) * PACK], BF16, name="grouped", tag=tag, align_bytes=64)
            engine.tensor_tensor(
                grouped[:].rearrange("p (c i t) -> p c t i", i=4, t=PACK),
                h1[:, :, m0:m1].rearrange("p t (c i) -> p c t i", i=4),
                h2[:, :, m0:m1].rearrange("p t (c i) -> p c t i", i=4),
                op,
            )
            return grouped

        h1 = work.tile([P, PACK, PAIRS], F32, name="h1", tag="h1")
        h2 = work.tile([P, PACK, PAIRS], F32, name="h2", tag="h2")
        accs = [[bank(2 * t + half) for half in range(2)] for t in range(PACK)]
        for a, t in [(0, 0), (0, 1), (0, 2), (0, 3), (1, 0), (1, 1), (2, 0), (2, 1), (1, 2), (2, 2), (1, 3), (2, 3)]:
            for half in range(2):
                first_pass(accs[t][half], a, 0, t, half)
        rounded = []
        for t in range(2):
            pick(features(accs[t], 0, t, keep, f"gate{t}"), h1, h2, t)
            rounded.append(round_w1_on_gpsimd(load_w1(t, 1), f"gate{t}"))
        pick(features(accs[2], 0, 2), h1, h2, 2)
        quantize_w1(0, 1, 0, rounded[0], "h02")
        quantize_w1(1, 1, 0, rounded[1])
        pick(features(accs[3], 0, 3), h1, h2, 3)
        quantize_w1(2, 1, 0, round_w1(load_w1(2, 1), 0, PACK, nc.scalar.copy, "chain", keep))

        hs = []
        for t in range(PACK):
            accs = [bank(2 * t + half) for half in range(2)]
            for a in range(K_PASSES):
                for half in range(2):
                    first_pass(accs[half], a, 1, t, half)
            hs.append(features(accs, 1, t))
        low0 = quantize(combine(ALU.min, h1, h2, 0, PAIRS, keep, "chain"), "low0")
        diff0 = combine(ALU.subtract, h1, h2, 0, PAIRS, keep, "chain", nc.gpsimd)

        wm_grouped = keep.tile([P, H_PASSES, N * PACK], BF16, name="wm_grouped", align_bytes=64)
        for b in range(H_PASSES):
            raw = load_rows(wm[K_PASS * b : K_PASS * (b + 1), :])
            nc.scalar.copy(
                wm_grouped[:, b, :].rearrange("p (c i j) -> p c j i", i=4, j=PACK),
                raw[:].rearrange("p j (c i) -> p c j i", i=4),
            )
        wd_codes = stage.tile([P, H_PASSES, 2 * N], U8, name="wd_codes", tag="raw", align_bytes=64)
        nc.sync.dma_start(out=wd_codes[:].bitcast(I32), in_=wd_words.rearrange("b p c -> p b c").bitcast(I32))
        wd_planes = stage.tile([P, H_PASSES, N], U8, name="wd_planes", tag="raw", align_bytes=64)
        nc.gpsimd.memset(wd_planes[:].bitcast(I32), 0)
        for d in range(4):
            nc.sync.dma_start(
                out=wd_planes[32 * d : 32 * d + 4].bitcast(I32),
                in_=wd_scales[:, 4 * d : 4 * d + 4, :].rearrange("b r c -> r b c").bitcast(I32),
            )

        h1 = work.tile([P, PACK, PAIRS], F32, name="h1", tag="h1")
        h2 = work.tile([P, PACK, PAIRS], F32, name="h2", tag="h2")
        for t in range(PACK):
            pick(hs[t], h1, h2, t)
            if t == 2:
                diff0 = quantize(diff0, "diff0", "h12")

        wm_codes = keep.tile([P, H_PASSES * N], U32, name="wm_codes", tag="chain", align_bytes=64)
        wm_planes = keep.tile([P, H_PASSES * N], U8, name="wm_planes", align_bytes=64)
        wm_flat = wm_grouped[:].rearrange("p b c -> p (b c)")
        for c0, c1 in ((0, 512), (512, 768)):
            nc.vector.quantize_mx(
                out=wm_codes[:, c0:c1].bitcast(FP8X4), scales=wm_planes[:, c0:c1], in_=wm_flat[:, PACK * c0 : PACK * c1]
            )

        def diff_passes(acc_diff, b, diff):
            for u in range(N_SLICES):
                nc.tensor.matmul_mx(
                    out=acc_diff[:, P * u : P * (u + 1)],
                    lhsT=wd_codes[:, b, 2 * P * u : 2 * P * (u + 1)].bitcast(FP4X4),
                    lhsT_scale=wd_planes[:, b, P * u : P * (u + 1)],
                    rhs=diff[0].bitcast(FP8X4),
                    rhs_scale=diff[1],
                    start=(b == 0 and u == 0),
                    stop=(b == H_PASSES - 1 and u == N_SLICES - 1),
                )

        def low_passes(acc_low, b, low):
            for u in range(N_SLICES):
                cols = slice(N * b + P * u, N * b + P * (u + 1))
                nc.tensor.matmul_mx(
                    out=acc_low[:, P * u : P * (u + 1)],
                    lhsT=wm_codes[:, cols].bitcast(FP8X4),
                    lhsT_scale=wm_planes[:, cols],
                    rhs=low[0].bitcast(FP8X4),
                    rhs_scale=low[1],
                    start=(b == 0 and u == 0),
                    stop=(b == H_PASSES - 1 and u == N_SLICES - 1),
                )

        chunks = PAIRS // CHUNK
        sums = [(bank(2 * q), bank(2 * q + 1)) for q in range(chunks)]
        for q in range(chunks):
            c0, c1 = CHUNK * q, CHUNK * (q + 1)
            diff_passes(sums[q][0], 0, columns(diff0, c0, c1))
            low_passes(sums[q][1], 0, columns(low0, c0, c1))

        out_view = out.rearrange("(u p) m -> p u m", p=P)
        logs = {}

        def finish_diff(grouped, q0, q1):
            diff = quantize(grouped, f"diff1_{q0}")
            for q in range(q0, q1):
                diff_passes(sums[q][0], 1, columns(diff, CHUNK * (q - q0), CHUNK * (q - q0 + 1)))
                size = work.tile([P, N], F32, name="size", tag="size")
                nc.scalar.activation(size[:], sums[q][0][:, :N], ACT.Abs)
                logs[q] = keep.tile([P, N], F32, name=f"logs{q}")
                nc.scalar.activation(logs[q][:], size[:], ACT.Ln, bias=1.0)

        def finish_low(grouped, q0, q1):
            low = quantize(grouped, f"low1_{q0}")
            for q in range(q0, q1):
                low_passes(sums[q][1], 1, columns(low, CHUNK * (q - q0), CHUNK * (q - q0 + 1)))

        def pairs(op, q0, q1):
            return combine(op, h1, h2, CHUNK * q0, CHUNK * q1, keep, f"pairs{q0}_{op == ALU.min}")

        def store(q):
            scores = keep.tile([P, N], F32, name=f"scores{q}")
            nc.vector.tensor_tensor(scores[:], sums[q][1][:, :N], logs[q][:], ALU.add)
            nc.sync.dma_start(
                out=out_view[:, :, CHUNK * q : CHUNK * (q + 1)],
                in_=scores[:].rearrange("p (u m) -> p u m", m=CHUNK),
            )

        for q0, q1 in ((0, 2), (2, 3)):
            diff, low = pairs(ALU.subtract, q0, q1), pairs(ALU.min, q0, q1)
            finish_diff(diff, q0, q1)
            finish_low(low, q0, q1)
        store(0)
        diff = pairs(ALU.subtract, 3, 4)
        store(1)
        finish_diff(diff, 3, 4)
        low = pairs(ALU.min, 3, 4)
        store(2)
        finish_low(low, 3, 4)
        store(3)
